import numpy as np
import ml_dtypes


def mxq(x, axis, fmt="e4m3"):
    dtype, down = {"e4m3": (ml_dtypes.float8_e4m3fn, 7), "e5m2": (ml_dtypes.float8_e5m2, 14)}[fmt]
    v = np.moveaxis(np.asarray(x, np.float32).astype(ml_dtypes.bfloat16).astype(np.float64), axis, -1)
    blocks = v.reshape(v.shape[:-1] + (-1, 32))
    amax = np.abs(blocks).max(-1, keepdims=True)
    byte = np.maximum(np.where(amax > 0, np.frexp(amax)[1] - 1 + 127, 0) - down, 1)
    scale = np.exp2(byte - 127.0)
    codes = (blocks / scale).astype(np.float32).astype(dtype).astype(np.float64)
    return np.moveaxis((codes * scale).reshape(v.shape), -1, axis)


WIDE = False


def mx_kscale(k):
    if not WIDE:
        return np.ones(k)
    levels = np.array([10, -10, 5, -5, 0])
    if k % 512:
        return np.exp2(np.random.permutation(np.resize(levels, k // 32))).repeat(32)
    a = np.empty((k // 512, 16))
    for p in range(k // 512):
        a[p, :8] = np.random.permutation(np.resize(levels, 8))
        for g in range(8):
            far = levels[np.abs(levels - a[p, g]) >= 10]
            a[p, g + 8] = far[np.random.randint(len(far))]
    return np.exp2(a.ravel()).repeat(32)


def f64(x):
    return np.asarray(x).astype(np.float64)


def striped(idx):
    return np.tile(idx.reshape(-1, 16).T, (8, 1)).astype(np.uint16)


def unstriped(offs):
    return offs[:16].T.reshape(-1).astype(np.int64)


def striped8(idx):
    return np.concatenate([x.reshape(-1, 16).T for x in idx]).astype(np.uint16)


def runs(offs, k):
    lists = np.stack([offs[16 * r : 16 * r + 16].T.reshape(-1) for r in range(8)]).astype(np.int64)
    return lists[np.arange(k) % 512 // 64]


def pack_weight(w):
    k, n = w.shape
    w = f64(np.asarray(w, np.float32).astype(ml_dtypes.bfloat16)).reshape(k // 32, 32, n)
    amax = np.abs(w).max(1)
    byte = np.clip(np.where(amax > 0, np.frexp(amax)[1] - 1 + 127 - 7, 1), 1, 254)
    scaled = (w * np.exp2(127.0 - byte)[:, None, :]).reshape(k, n).astype(np.float32)
    words = np.ascontiguousarray(scaled.reshape(k // 512, 128, 4, n).transpose(0, 1, 3, 2)).astype(ml_dtypes.float8_e4m3fn).view(np.uint8)
    return words, np.ascontiguousarray(byte.astype(np.uint8).reshape(k // 512, 16, n))


def unpack_weight(words, scales):
    g, p, n, _ = words.shape
    vals = np.ascontiguousarray(words).view(ml_dtypes.float8_e4m3fn).astype(np.float64) * np.repeat(np.exp2(scales.astype(np.float64) - 127.0), 8, axis=1)[..., None]
    return vals.transpose(0, 1, 3, 2).reshape(g * 512, n)


E2M1 = np.array([0.0, 0.5, 1.0, 1.5, 2.0, 3.0, 4.0, 6.0, -0.0, -0.5, -1.0, -1.5, -2.0, -3.0, -4.0, -6.0])


def pack_fp4(w):
    k, n = w.shape
    w = f64(np.asarray(w, np.float32).astype(ml_dtypes.bfloat16)).reshape(k // 32, 32, n)
    amax = np.abs(w).max(1)
    mant, ex = np.frexp(amax / 6.0)
    byte = np.clip(np.where(amax > 0, np.where(mant > 0.5, ex, ex - 1) + 127, 1), 1, 254)
    scaled = (w * np.exp2(127.0 - byte)[:, None, :]).reshape(k, n).astype(np.float32)
    c = np.ascontiguousarray(scaled.reshape(k // 512, 128, 4, n).transpose(0, 1, 3, 2)).astype(ml_dtypes.float4_e2m1fn).view(np.uint8) & 0xF
    words = (c[..., 0::2] | (c[..., 1::2] << 4)).reshape(k // 512, 128, 2 * n)
    return np.ascontiguousarray(words), np.ascontiguousarray(byte.astype(np.uint8).reshape(k // 512, 16, n))


def unpack_fp4(words, scales):
    g, _, n = scales.shape
    words = np.ascontiguousarray(words).reshape(g, 128, n, 2)
    nib = np.empty((g, 128, n, 4), np.uint8)
    nib[..., 0::2] = words & 0xF
    nib[..., 1::2] = words >> 4
    vals = E2M1[nib] * np.repeat(np.exp2(scales.astype(np.float64) - 127.0), 8, axis=1)[..., None]
    return vals.transpose(0, 1, 3, 2).reshape(g * 512, n)


def relu(v):
    return np.maximum(v, 0.0)

def planes(y):
    n, m = y.shape
    v = y.astype(np.float32).astype(ml_dtypes.bfloat16).astype(np.float64).reshape(n // 32, 32, m)
    top = np.abs(v).max(1)
    byte = np.clip(np.where(top > 0, np.frexp(top)[1] - 1 + 127 - 7, 1), 1, 254)
    codes = (v * np.exp2(127.0 - byte)[:, None, :]).reshape(n, m).astype(np.float32).astype(ml_dtypes.float8_e4m3fn).view(np.uint8)
    words = codes.reshape(n // 512, 128, 4, m).transpose(0, 1, 3, 2)
    return np.ascontiguousarray(words), np.ascontiguousarray(byte.astype(np.uint8).reshape(n // 512, 16, m))


K, T, S, H, C = 512, 2048, 512, 512, 512


def setup_inputs():
    n = np.random.standard_normal
    s = mx_kscale(K)[:, None]
    packed_xT = pack_weight(n((K, T)) * s)
    packed_w1 = pack_fp4(n((K, H)) / np.sqrt(K) / s)
    return {
        "x_words": packed_xT[0],
        "x_scales": packed_xT[1],
        "w1_words": packed_w1[0],
        "w1_scales": packed_w1[1],
        "gs": (np.random.uniform(0.5, 1.5, (K, 1)) / s).astype(np.float32),
        "offs": striped(np.random.permutation(T)[:S]),
        "cand": striped(np.random.permutation(T)[:C]),
        "n1": striped8(np.stack([np.random.permutation(S) for _ in range(8)])),
        "n2": striped8(np.stack([np.random.permutation(S) for _ in range(8)])),
        "n3": striped8(np.stack([np.random.permutation(S) for _ in range(8)])),
    }


def reference(x_words, x_scales, w1_words, w1_scales, gs, offs, cand, n1, n2, n3):
    x_cand = unpack_weight(x_words, x_scales)[:, unstriped(cand)]
    xq = unpack_weight(x_words, x_scales)[:, unstriped(offs)]
    h = relu(unpack_fp4(w1_words, w1_scales).T @ xq)
    z = f64(gs) * h
    s = 0.0625 * ((x_cand.T @ mxq(z, 0, "e4m3")))
    ex = np.exp(0.5 * s)
    out_0 = np.log((ex + ex[np.arange(C)[:, None], runs(n1, C)]) / (ex[np.arange(C)[:, None], runs(n2, C)] + ex[np.arange(C)[:, None], runs(n3, C)]))
    return (out_0,) + planes(out_0)

@@ -1,0 +1,194 @@
+from contextlib import ExitStack
+
+import concourse.mybir as mybir
+
+K, T, S, H, C = 512, 2048, 512, 512, 512
+FLOPS = 2 * K * H * S + 2 * K * C * S
+
+F32 = mybir.dt.float32
+BF16 = mybir.dt.bfloat16
+I32 = mybir.dt.int32
+U32 = mybir.dt.uint32
+U16 = mybir.dt.uint16
+U8 = mybir.dt.uint8
+FP8X4 = mybir.dt.float8_e4m3fn_x4
+FP4X4 = mybir.dt.float4_e2m1fn_x4
+ALU = mybir.AluOpType
+ACT = mybir.ActivationFunctionType
+
+P = 128
+PACK = 4
+QUADS = 4
+ZW = 128
+HALF = 256
+OUT_CHUNKS = ((0, 256), (256, 128), (384, 128))
+
+
+def tile_picked_candodds_none_po_kernel(
+    tc, x_words, x_scales, w1_words, w1_scales, gs, offs, cand, n1, n2, n3, out_0, out_1, out_2
+):
+    nc = tc.nc
+    with ExitStack() as ctx:
+        keep = ctx.enter_context(tc.tile_pool(name="keep", bufs=1))
+        psum = ctx.enter_context(tc.psum_pool(name="psum", bufs=1))
+
+        def entries(lst, first, count):
+            return lst[:, first // 16 : (first + count) // 16]
+
+        offs_l = keep.tile([P, S // 16], U16, name="offs_l")
+        cand_l = keep.tile([P, C // 16], U16, name="cand_l")
+        n1_l = keep.tile([P, S // 16], U16, name="n1_l")
+        n2_l = keep.tile([P, S // 16], U16, name="n2_l")
+        n3_l = keep.tile([P, S // 16], U16, name="n3_l")
+        xw = keep.tile([P, T], U32, name="xw", align_bytes=64)
+        xs = keep.tile([P, T], U8, name="xs", align_bytes=64)
+        w_raw = keep.tile([P, 2 * H], U8, name="w_raw", align_bytes=64)
+        ws_raw = keep.tile([P, H], U8, name="ws_raw", align_bytes=64)
+        gs_sb = keep.tile([P, PACK], F32, name="gs_sb")
+
+        nc.vector.memset(xs[:].bitcast(I32), 0)
+        nc.vector.memset(ws_raw[:].bitcast(I32), 0)
+
+        nc.sync.dma_start(offs_l[:], offs)
+        nc.sync.dma_start(cand_l[:], cand)
+        for q in range(QUADS):
+            nc.scalar.dma_start(xs[32 * q : 32 * q + 4, :].bitcast(I32), x_scales[0, 4 * q : 4 * q + 4, :].bitcast(I32))
+        nc.sync.dma_start(xw[:].bitcast(I32), x_words[0].rearrange("p n t -> p (n t)").bitcast(I32))
+        nc.sync.dma_start(w_raw[:].bitcast(I32), w1_words[0].bitcast(I32))
+        for q in range(QUADS):
+            nc.sync.dma_start(ws_raw[32 * q : 32 * q + 4, :].bitcast(I32), w1_scales[0, 4 * q : 4 * q + 4, :].bitcast(I32))
+        nc.sync.dma_start(gs_sb[:], gs.rearrange("(p t) o -> p (t o)", t=PACK))
+        nc.sync.dma_start(n1_l[:], n1)
+        nc.sync.dma_start(n2_l[:], n2)
+        nc.sync.dma_start(n3_l[:], n3)
+
+        w_dealt = keep.tile([P, PACK, 2 * P], U8, name="w_dealt", align_bytes=64)
+        ws_dealt = keep.tile([P, PACK, P], U8, name="ws_dealt", align_bytes=64)
+        nc.scalar.copy(w_dealt[:].bitcast(U16), w_raw[:].bitcast(U16).rearrange("p (m t) -> p t m", t=PACK))
+
+        tok_s = keep.tile([P, S], U8, name="tok_s", align_bytes=64)
+        cand_s = keep.tile([P, PACK, P], U8, name="cand_s", align_bytes=64)
+        tok_w = keep.tile([P, S], U32, name="tok_w", align_bytes=64)
+        cand_w = keep.tile([P, PACK, P], U32, name="cand_w", align_bytes=64)
+        nc.vector.tensor_copy(tok_s[:], xs[:].indirect(offs_l[:]))
+        nc.vector.tensor_copy(ws_dealt[:], ws_raw[:].rearrange("p (m t) -> p t m", t=PACK))
+        nc.vector.tensor_copy(cand_s[:].rearrange("p t m -> p m t"), xs[:].indirect(cand_l[:]))
+        for h0 in range(0, S, HALF):
+            nc.vector.tensor_copy(tok_w[:, h0 : h0 + HALF], xw[:].indirect(entries(offs_l, h0, HALF)))
+        nc.vector.tensor_copy(cand_w[:].rearrange("p t m -> p m t"), xw[:].indirect(cand_l[:]))
+
+        n_z = S // ZW
+        h_ps = []
+        for c in range(n_z):
+            cols = slice(c * ZW, (c + 1) * ZW)
+            bank = psum.tile([P, PACK, ZW], F32, name=f"h_ps{c}", tag=f"bank{c}")
+            for t in range(PACK):
+                nc.tensor.matmul_mx(
+                    out=bank[:, t, :],
+                    lhsT=w_dealt[:, t, :].bitcast(FP4X4),
+                    lhsT_scale=ws_dealt[:, t, :],
+                    rhs=tok_w[:, cols].bitcast(FP8X4),
+                    rhs_scale=tok_s[:, cols],
+                    start=True,
+                    stop=True,
+                )
+            h_ps.append(bank)
+
+        z_bf = [keep.tile([P, ZW, PACK], BF16, name=f"z_bf{c}", align_bytes=64) for c in range(n_z)]
+        z_w = [keep.tile([P, HALF], U32, name=f"z_w{h}", align_bytes=64) for h in range(2)]
+        z_s = [keep.tile([P, HALF], U8, name=f"z_s{h}", align_bytes=64) for h in range(2)]
+        ex = [keep.tile([P, S], F32, name=f"ex{t}", align_bytes=64) for t in range(PACK)]
+        ex_plain = [keep.tile([P, S], F32, name=f"ex_plain{t}", align_bytes=64) for t in range(PACK)]
+
+        def weigh(c):
+            nc.vector.scalar_tensor_tensor(
+                out=z_bf[c][:],
+                in0=h_ps[c][:].rearrange("p t n -> p n t"),
+                scalar=0.0,
+                in1=gs_sb[:].unsqueeze(1).to_broadcast([P, ZW, PACK]),
+                op0=ALU.max,
+                op1=ALU.mult,
+            )
+
+        def quantise_z(c):
+            h, part = divmod(c * ZW, HALF)
+            nc.vector.quantize_mx(
+                out=z_w[h][:, part : part + ZW].bitcast(FP8X4),
+                scales=z_s[h][:, part : part + ZW],
+                in_=z_bf[c][:].rearrange("p n t -> p (n t)"),
+            )
+
+        def score(h):
+            cols = slice(h * HALF, (h + 1) * HALF)
+            for t in range(PACK):
+                bank = psum.tile([P, HALF], F32, name=f"s_ps{h}{t}", tag=f"bank{(1 - h) * PACK + t}")
+                nc.tensor.matmul_mx(
+                    out=bank[:],
+                    lhsT=cand_w[:, t, :].bitcast(FP8X4),
+                    lhsT_scale=cand_s[:, t, :],
+                    rhs=z_w[h][:].bitcast(FP8X4),
+                    rhs_scale=z_s[h][:],
+                    start=True,
+                    stop=True,
+                )
+                nc.scalar.activation(out=ex[t][:, cols], in_=bank[:], func=ACT.Exp, scale=0.5 * 0.0625)
+                nc.sync.dma_start(ex_plain[t][:, cols], ex[t][:, cols])
+
+        weigh(0)
+        weigh(1)
+        quantise_z(0)
+        weigh(2)
+        quantise_z(1)
+        score(0)
+        weigh(3)
+        quantise_z(2)
+        quantise_z(3)
+        score(1)
+
+        y_w = keep.tile([P, S], U32, name="y_w", align_bytes=64)
+        y_s = keep.tile([P, S], U8, name="y_s", align_bytes=64)
+        out_rows = out_0.rearrange("(p t) j -> p t j", t=PACK)
+        out_words = out_1[0].rearrange("p n t -> p (n t)").bitcast(I32)
+
+        logs = {}
+
+        def fetch(i):
+            j0, w = OUT_CHUNKS[i]
+            num = keep.tile([P, PACK, w], F32, name=f"num{i}", align_bytes=64)
+            den = keep.tile([P, PACK, w], F32, name=f"den{i}", align_bytes=64)
+            at2 = keep.tile([P, PACK, w], F32, name=f"at2_{i}", align_bytes=64)
+            for t in range(PACK):
+                nc.scalar.activation(out=at2[:, t, :], in_=ex[t][:].indirect(entries(n2_l, j0, w)), func=ACT.Copy)
+            for t in range(PACK):
+                nc.vector.tensor_tensor(num[:, t, :], ex[t][:].indirect(entries(n1_l, j0, w)), ex_plain[t][:, j0 : j0 + w], ALU.add)
+            for t in range(PACK):
+                nc.vector.tensor_tensor(den[:, t, :], ex[t][:].indirect(entries(n3_l, j0, w)), at2[:, t, :], ALU.add)
+            ln_num = keep.tile([P, PACK, w], F32, name=f"ln_num{i}", align_bytes=64)
+            ln_den = keep.tile([P, PACK, w], F32, name=f"ln_den{i}", align_bytes=64)
+            nc.scalar.activation(out=ln_num[:], in_=num[:], func=ACT.Ln)
+            nc.scalar.activation(out=ln_den[:], in_=den[:], func=ACT.Ln)
+            logs[i] = (ln_num, ln_den)
+
+        def hand_out(i):
+            j0, w = OUT_CHUNKS[i]
+            ln_num, ln_den = logs[i]
+            y = keep.tile([P, PACK, w], F32, name=f"y{i}", align_bytes=64)
+            y_bf = keep.tile([P, w, PACK], BF16, name=f"y_bf{i}", align_bytes=64)
+            nc.vector.tensor_tensor(y[:], ln_num[:], ln_den[:], ALU.subtract)
+            nc.sync.dma_start(out_rows[:, :, j0 : j0 + w], y[:])
+            nc.vector.tensor_copy(y_bf[:], y[:].rearrange("p t j -> p j t"))
+            nc.vector.quantize_mx(
+                out=y_w[:, j0 : j0 + w].bitcast(FP8X4),
+                scales=y_s[:, j0 : j0 + w],
+                in_=y_bf[:].rearrange("p j t -> p (j t)"),
+            )
+            nc.sync.dma_start(out_words[:, j0 : j0 + w], y_w[:, j0 : j0 + w].bitcast(I32))
+
+        fetch(0)
+        for i in range(1, len(OUT_CHUNKS)):
+            fetch(i)
+            hand_out(i - 1)
+        hand_out(len(OUT_CHUNKS) - 1)
+        for q in range(QUADS):
+            eng = nc.sync if q % 2 == 0 else nc.scalar
+            eng.dma_start(out_2[0, 4 * q : 4 * q + 4, :].bitcast(I32), y_s[32 * q : 32 * q + 4, :].bitcast(I32))

@@ -46,15 +46,16 @@ def tile_picked_candodds_none_po_kernel(
         ws_raw = keep.tile([P, H], U8, name="ws_raw", align_bytes=64)
         gs_sb = keep.tile([P, PACK], F32, name="gs_sb")
 
-        nc.vector.memset(xs[:].bitcast(I32), 0)
-        nc.vector.memset(ws_raw[:].bitcast(I32), 0)
+        nc.vector.memset(xs[:, : T // 2].bitcast(I32), 0)
+        nc.gpsimd.memset(xs[:, T // 2 :].bitcast(I32), 0)
+        nc.gpsimd.memset(ws_raw[:].bitcast(I32), 0)
 
         nc.sync.dma_start(offs_l[:], offs)
         nc.sync.dma_start(cand_l[:], cand)
-        for q in range(QUADS):
-            nc.scalar.dma_start(xs[32 * q : 32 * q + 4, :].bitcast(I32), x_scales[0, 4 * q : 4 * q + 4, :].bitcast(I32))
-        nc.sync.dma_start(xw[:].bitcast(I32), x_words[0].rearrange("p n t -> p (n t)").bitcast(I32))
         nc.sync.dma_start(w_raw[:].bitcast(I32), w1_words[0].bitcast(I32))
+        for q in range(QUADS):
+            nc.sync.dma_start(xs[32 * q : 32 * q + 4, :].bitcast(I32), x_scales[0, 4 * q : 4 * q + 4, :].bitcast(I32))
+        nc.sync.dma_start(xw[:].bitcast(I32), x_words[0].rearrange("p n t -> p (n t)").bitcast(I32))
         for q in range(QUADS):
             nc.sync.dma_start(ws_raw[32 * q : 32 * q + 4, :].bitcast(I32), w1_scales[0, 4 * q : 4 * q + 4, :].bitcast(I32))
         nc.sync.dma_start(gs_sb[:], gs.rearrange("(p t) o -> p (t o)", t=PACK))
@@ -71,10 +72,10 @@ def tile_picked_candodds_none_po_kernel(
         tok_w = keep.tile([P, S], U32, name="tok_w", align_bytes=64)
         cand_w = keep.tile([P, PACK, P], U32, name="cand_w", align_bytes=64)
         nc.vector.tensor_copy(tok_s[:], xs[:].indirect(offs_l[:]))
-        nc.vector.tensor_copy(ws_dealt[:], ws_raw[:].rearrange("p (m t) -> p t m", t=PACK))
         nc.vector.tensor_copy(cand_s[:].rearrange("p t m -> p m t"), xs[:].indirect(cand_l[:]))
-        for h0 in range(0, S, HALF):
-            nc.vector.tensor_copy(tok_w[:, h0 : h0 + HALF], xw[:].indirect(entries(offs_l, h0, HALF)))
+        nc.gpsimd.tensor_copy(ws_dealt[:], ws_raw[:].rearrange("p (m t) -> p t m", t=PACK))
+        for first, count in ((0, ZW), (ZW, S - ZW)):
+            nc.vector.tensor_copy(tok_w[:, first : first + count], xw[:].indirect(entries(offs_l, first, count)))
         nc.vector.tensor_copy(cand_w[:].rearrange("p t m -> p m t"), xw[:].indirect(cand_l[:]))
 
         n_z = S // ZW
@@ -110,6 +111,14 @@ def tile_picked_candodds_none_po_kernel(
                 op1=ALU.mult,
             )
 
+        def weigh_on_scalar(c):
+            h_pos = keep.tile([P, PACK, ZW], F32, name=f"h_pos{c}", align_bytes=64)
+            z_rows = keep.tile([P, PACK, ZW], BF16, name=f"z_rows{c}", align_bytes=64)
+            nc.scalar.activation(out=h_pos[:], in_=h_ps[c][:], func=ACT.Relu)
+            for t in range(PACK):
+                nc.scalar.activation(out=z_rows[:, t, :], in_=h_pos[:, t, :], func=ACT.Copy, scale=gs_sb[:, t : t + 1])
+            nc.scalar.copy(z_bf[c][:], z_rows[:].rearrange("p t n -> p n t"))
+
         def quantise_z(c):
             h, part = divmod(c * ZW, HALF)
             nc.vector.quantize_mx(
@@ -132,17 +141,20 @@ def tile_picked_candodds_none_po_kernel(
                     stop=True,
                 )
                 nc.scalar.activation(out=ex[t][:, cols], in_=bank[:], func=ACT.Exp, scale=0.5 * 0.0625)
-                nc.sync.dma_start(ex_plain[t][:, cols], ex[t][:, cols])
+                if h == 1:
+                    nc.sync.dma_start(ex_plain[t][:, cols], ex[t][:, cols])
 
-        weigh(0)
+        weigh_on_scalar(0)
         weigh(1)
-        quantise_z(0)
         weigh(2)
         quantise_z(1)
+        quantise_z(0)
         score(0)
         weigh(3)
         quantise_z(2)
         quantise_z(3)
+        for t in range(PACK):
+            nc.vector.tensor_copy(ex_plain[t][:, :HALF], ex[t][:, :HALF])
         score(1)
 
         y_w = keep.tile([P, S], U32, name="y_w", align_bytes=64)

@@ -21,7 +21,6 @@ PACK = 4
 QUADS = 4
 ZW = 128
 HALF = 256
-OUT_CHUNKS = ((0, 256), (256, 128), (384, 128))
 
 
 def tile_picked_candodds_none_po_kernel(
@@ -74,13 +73,13 @@ def tile_picked_candodds_none_po_kernel(
         nc.vector.tensor_copy(tok_s[:], xs[:].indirect(offs_l[:]))
         nc.vector.tensor_copy(cand_s[:].rearrange("p t m -> p m t"), xs[:].indirect(cand_l[:]))
         nc.gpsimd.tensor_copy(ws_dealt[:], ws_raw[:].rearrange("p (m t) -> p t m", t=PACK))
-        for first, count in ((0, ZW), (ZW, S - ZW)):
+        for first, count in ((S - ZW, ZW), (0, S - ZW)):
             nc.vector.tensor_copy(tok_w[:, first : first + count], xw[:].indirect(entries(offs_l, first, count)))
         nc.vector.tensor_copy(cand_w[:].rearrange("p t m -> p m t"), xw[:].indirect(cand_l[:]))
 
         n_z = S // ZW
-        h_ps = []
-        for c in range(n_z):
+        h_ps = {}
+        for c in (n_z - 1, *range(n_z - 1)):
             cols = slice(c * ZW, (c + 1) * ZW)
             bank = psum.tile([P, PACK, ZW], F32, name=f"h_ps{c}", tag=f"bank{c}")
             for t in range(PACK):
@@ -93,7 +92,7 @@ def tile_picked_candodds_none_po_kernel(
                     start=True,
                     stop=True,
                 )
-            h_ps.append(bank)
+            h_ps[c] = bank
 
         z_bf = [keep.tile([P, ZW, PACK], BF16, name=f"z_bf{c}", align_bytes=64) for c in range(n_z)]
         z_w = [keep.tile([P, HALF], U32, name=f"z_w{h}", align_bytes=64) for h in range(2)]
@@ -117,7 +116,7 @@ def tile_picked_candodds_none_po_kernel(
             nc.scalar.activation(out=h_pos[:], in_=h_ps[c][:], func=ACT.Relu)
             for t in range(PACK):
                 nc.scalar.activation(out=z_rows[:, t, :], in_=h_pos[:, t, :], func=ACT.Copy, scale=gs_sb[:, t : t + 1])
-            nc.scalar.copy(z_bf[c][:], z_rows[:].rearrange("p t n -> p n t"))
+            nc.scalar.copy(z_bf[c][:].rearrange("p (c i) t -> p c t i", i=4), z_rows[:].rearrange("p t (c i) -> p c t i", i=4))
 
         def quantise_z(c):
             h, part = divmod(c * ZW, HALF)
@@ -144,15 +143,15 @@ def tile_picked_candodds_none_po_kernel(
                 if h == 1:
                     nc.sync.dma_start(ex_plain[t][:, cols], ex[t][:, cols])
 
-        weigh_on_scalar(0)
+        weigh_on_scalar(3)
+        weigh(0)
         weigh(1)
-        weigh(2)
-        quantise_z(1)
         quantise_z(0)
+        quantise_z(1)
         score(0)
-        weigh(3)
-        quantise_z(2)
+        weigh(2)
         quantise_z(3)
+        quantise_z(2)
         for t in range(PACK):
             nc.vector.tensor_copy(ex_plain[t][:, :HALF], ex[t][:, :HALF])
         score(1)
@@ -162,45 +161,68 @@ def tile_picked_candodds_none_po_kernel(
         out_rows = out_0.rearrange("(p t) j -> p t j", t=PACK)
         out_words = out_1[0].rearrange("p n t -> p (n t)").bitcast(I32)
 
-        logs = {}
+        ln_num = keep.tile([P, PACK, S], F32, name="ln_num", align_bytes=64)
+        ln_den = keep.tile([P, PACK, S], F32, name="ln_den", align_bytes=64)
 
-        def fetch(i):
-            j0, w = OUT_CHUNKS[i]
-            num = keep.tile([P, PACK, w], F32, name=f"num{i}", align_bytes=64)
-            den = keep.tile([P, PACK, w], F32, name=f"den{i}", align_bytes=64)
-            at2 = keep.tile([P, PACK, w], F32, name=f"at2_{i}", align_bytes=64)
+        def fetch_n2(h):
+            at2 = keep.tile([P, PACK, HALF], F32, name=f"at2_{h}", align_bytes=64)
             for t in range(PACK):
-                nc.scalar.activation(out=at2[:, t, :], in_=ex[t][:].indirect(entries(n2_l, j0, w)), func=ACT.Copy)
-            for t in range(PACK):
-                nc.vector.tensor_tensor(num[:, t, :], ex[t][:].indirect(entries(n1_l, j0, w)), ex_plain[t][:, j0 : j0 + w], ALU.add)
-            for t in range(PACK):
-                nc.vector.tensor_tensor(den[:, t, :], ex[t][:].indirect(entries(n3_l, j0, w)), at2[:, t, :], ALU.add)
-            ln_num = keep.tile([P, PACK, w], F32, name=f"ln_num{i}", align_bytes=64)
-            ln_den = keep.tile([P, PACK, w], F32, name=f"ln_den{i}", align_bytes=64)
-            nc.scalar.activation(out=ln_num[:], in_=num[:], func=ACT.Ln)
-            nc.scalar.activation(out=ln_den[:], in_=den[:], func=ACT.Ln)
-            logs[i] = (ln_num, ln_den)
+                nc.scalar.activation(out=at2[:, t, :], in_=ex[t][:].indirect(entries(n2_l, h * HALF, HALF)), func=ACT.Copy)
+            return at2
 
-        def hand_out(i):
-            j0, w = OUT_CHUNKS[i]
-            ln_num, ln_den = logs[i]
-            y = keep.tile([P, PACK, w], F32, name=f"y{i}", align_bytes=64)
-            y_bf = keep.tile([P, w, PACK], BF16, name=f"y_bf{i}", align_bytes=64)
-            nc.vector.tensor_tensor(y[:], ln_num[:], ln_den[:], ALU.subtract)
+        def numerators(h):
+            j0 = h * HALF
+            num = keep.tile([P, PACK, HALF], F32, name=f"num{h}", align_bytes=64)
+            for t in range(PACK):
+                nc.vector.tensor_tensor(num[:, t, :], ex[t][:].indirect(entries(n1_l, j0, HALF)), ex_plain[t][:, j0 : j0 + HALF], ALU.add)
+            return num
+
+        def denominators(h, at2):
+            den = keep.tile([P, PACK, HALF], F32, name=f"den{h}", align_bytes=64)
+            for t in range(PACK):
+                nc.vector.tensor_tensor(den[:, t, :], ex[t][:].indirect(entries(n3_l, h * HALF, HALF)), at2[:, t, :], ALU.add)
+            return den
+
+        def take_logs(ln, sums, j0, first, w):
+            nc.scalar.activation(out=ln[:, :, j0 + first : j0 + first + w], in_=sums[:, :, first : first + w], func=ACT.Ln)
+
+        def subtract(j0, w):
+            y = keep.tile([P, PACK, w], F32, name=f"y{j0}", align_bytes=64)
+            nc.vector.tensor_tensor(y[:], ln_num[:, :, j0 : j0 + w], ln_den[:, :, j0 : j0 + w], ALU.subtract)
             nc.sync.dma_start(out_rows[:, :, j0 : j0 + w], y[:])
-            nc.vector.tensor_copy(y_bf[:], y[:].rearrange("p t j -> p j t"))
+            return y
+
+        def interleave(copy, y_bf, y):
+            copy(y_bf.rearrange("p (c i) t -> p c t i", i=4), y.rearrange("p t (c i) -> p c t i", i=4))
+
+        def quantise_y(y_bf, j0):
             nc.vector.quantize_mx(
-                out=y_w[:, j0 : j0 + w].bitcast(FP8X4),
-                scales=y_s[:, j0 : j0 + w],
+                out=y_w[:, j0 : j0 + HALF].bitcast(FP8X4),
+                scales=y_s[:, j0 : j0 + HALF],
                 in_=y_bf[:].rearrange("p j t -> p (j t)"),
             )
-            nc.sync.dma_start(out_words[:, j0 : j0 + w], y_w[:, j0 : j0 + w].bitcast(I32))
+            nc.sync.dma_start(out_words[:, j0 : j0 + HALF], y_w[:, j0 : j0 + HALF].bitcast(I32))
 
-        fetch(0)
-        for i in range(1, len(OUT_CHUNKS)):
-            fetch(i)
-            hand_out(i - 1)
-        hand_out(len(OUT_CHUNKS) - 1)
+        y_bf = [keep.tile([P, HALF, PACK], BF16, name=f"y_bf{h}", align_bytes=64) for h in range(2)]
+        at2 = [fetch_n2(h) for h in range(2)]
+        num0 = numerators(0)
+        den0 = denominators(0, at2[0])
+        den1 = denominators(1, at2[1])
+        num1 = numerators(1)
+        take_logs(ln_num, num0, 0, 0, HALF)
+        take_logs(ln_den, den0, 0, 0, HALF)
+        take_logs(ln_den, den1, HALF, 0, HALF)
+        take_logs(ln_num, num1, HALF, 0, ZW)
+        take_logs(ln_num, num1, HALF, ZW, ZW)
+        y0 = subtract(0, HALF)
+        interleave(nc.vector.tensor_copy, y_bf[0][:, :ZW, :], y0[:, :, :ZW])
+        y2 = subtract(HALF, ZW)
+        y3 = subtract(HALF + ZW, ZW)
+        interleave(nc.scalar.copy, y_bf[0][:, ZW:, :], y0[:, :, ZW:])
+        interleave(nc.scalar.copy, y_bf[1][:, :ZW, :], y2[:])
+        interleave(nc.vector.tensor_copy, y_bf[1][:, ZW:, :], y3[:])
+        quantise_y(y_bf[0], 0)
+        quantise_y(y_bf[1], HALF)
         for q in range(QUADS):
             eng = nc.sync if q % 2 == 0 else nc.scalar
             eng.dma_start(out_2[0, 4 * q : 4 * q + 4, :].bitcast(I32), y_s[32 * q : 32 * q + 4, :].bitcast(I32))

from contextlib import ExitStack

import concourse.mybir as mybir

K, T, S, H, C = 512, 2048, 512, 512, 512
FLOPS = 2 * K * H * S + 2 * K * C * S

F32 = mybir.dt.float32
BF16 = mybir.dt.bfloat16
I32 = mybir.dt.int32
U32 = mybir.dt.uint32
U16 = mybir.dt.uint16
U8 = mybir.dt.uint8
FP8X4 = mybir.dt.float8_e4m3fn_x4
FP4X4 = mybir.dt.float4_e2m1fn_x4
ALU = mybir.AluOpType
ACT = mybir.ActivationFunctionType

P = 128
PACK = 4
QUADS = 4
ZW = 128
HALF = 256


def tile_picked_candodds_none_po_kernel(
    tc, x_words, x_scales, w1_words, w1_scales, gs, offs, cand, n1, n2, n3, out_0, out_1, out_2
):
    nc = tc.nc
    with ExitStack() as ctx:
        keep = ctx.enter_context(tc.tile_pool(name="keep", bufs=1))
        psum = ctx.enter_context(tc.psum_pool(name="psum", bufs=1))

        def entries(lst, first, count):
            return lst[:, first // 16 : (first + count) // 16]

        offs_l = keep.tile([P, S // 16], U16, name="offs_l")
        cand_l = keep.tile([P, C // 16], U16, name="cand_l")
        n1_l = keep.tile([P, S // 16], U16, name="n1_l")
        n2_l = keep.tile([P, S // 16], U16, name="n2_l")
        n3_l = keep.tile([P, S // 16], U16, name="n3_l")
        xw = keep.tile([P, T], U32, name="xw", align_bytes=64)
        xs = keep.tile([P, T], U8, name="xs", align_bytes=64)
        w_raw = keep.tile([P, 2 * H], U8, name="w_raw", align_bytes=64)
        ws_raw = keep.tile([P, H], U8, name="ws_raw", align_bytes=64)
        gs_sb = keep.tile([P, PACK], F32, name="gs_sb")

        nc.vector.memset(xs[:, : T // 2].bitcast(I32), 0)
        nc.gpsimd.memset(xs[:, T // 2 :].bitcast(I32), 0)
        nc.gpsimd.memset(ws_raw[:].bitcast(I32), 0)

        nc.sync.dma_start(offs_l[:], offs)
        nc.sync.dma_start(cand_l[:], cand)
        nc.sync.dma_start(w_raw[:].bitcast(I32), w1_words[0].bitcast(I32))
        for q in range(QUADS):
            nc.sync.dma_start(xs[32 * q : 32 * q + 4, :].bitcast(I32), x_scales[0, 4 * q : 4 * q + 4, :].bitcast(I32))
        nc.sync.dma_start(xw[:].bitcast(I32), x_words[0].rearrange("p n t -> p (n t)").bitcast(I32))
        for q in range(QUADS):
            nc.sync.dma_start(ws_raw[32 * q : 32 * q + 4, :].bitcast(I32), w1_scales[0, 4 * q : 4 * q + 4, :].bitcast(I32))
        nc.sync.dma_start(gs_sb[:], gs.rearrange("(p t) o -> p (t o)", t=PACK))
        nc.sync.dma_start(n1_l[:], n1)
        nc.sync.dma_start(n2_l[:], n2)
        nc.sync.dma_start(n3_l[:], n3)

        w_dealt = keep.tile([P, PACK, 2 * P], U8, name="w_dealt", align_bytes=64)
        ws_dealt = keep.tile([P, PACK, P], U8, name="ws_dealt", align_bytes=64)
        nc.scalar.copy(w_dealt[:].bitcast(U16), w_raw[:].bitcast(U16).rearrange("p (m t) -> p t m", t=PACK))

        tok_s = keep.tile([P, S], U8, name="tok_s", align_bytes=64)
        cand_s = keep.tile([P, PACK, P], U8, name="cand_s", align_bytes=64)
        tok_w = keep.tile([P, S], U32, name="tok_w", align_bytes=64)
        cand_w = keep.tile([P, PACK, P], U32, name="cand_w", align_bytes=64)
        nc.vector.tensor_copy(tok_s[:], xs[:].indirect(offs_l[:]))
        nc.vector.tensor_copy(cand_s[:].rearrange("p t m -> p m t"), xs[:].indirect(cand_l[:]))
        nc.gpsimd.tensor_copy(ws_dealt[:], ws_raw[:].rearrange("p (m t) -> p t m", t=PACK))
        for first, count in ((S - ZW, ZW), (0, S - ZW)):
            nc.vector.tensor_copy(tok_w[:, first : first + count], xw[:].indirect(entries(offs_l, first, count)))
        nc.vector.tensor_copy(cand_w[:].rearrange("p t m -> p m t"), xw[:].indirect(cand_l[:]))

        n_z = S // ZW
        h_ps = {}
        for c in (n_z - 1, *range(n_z - 1)):
            cols = slice(c * ZW, (c + 1) * ZW)
            bank = psum.tile([P, PACK, ZW], F32, name=f"h_ps{c}", tag=f"bank{c}")
            for t in range(PACK):
                nc.tensor.matmul_mx(
                    out=bank[:, t, :],
                    lhsT=w_dealt[:, t, :].bitcast(FP4X4),
                    lhsT_scale=ws_dealt[:, t, :],
                    rhs=tok_w[:, cols].bitcast(FP8X4),
                    rhs_scale=tok_s[:, cols],
                    start=True,
                    stop=True,
                )
            h_ps[c] = bank

        z_bf = [keep.tile([P, ZW, PACK], BF16, name=f"z_bf{c}", align_bytes=64) for c in range(n_z)]
        z_w = [keep.tile([P, HALF], U32, name=f"z_w{h}", align_bytes=64) for h in range(2)]
        z_s = [keep.tile([P, HALF], U8, name=f"z_s{h}", align_bytes=64) for h in range(2)]
        ex = [keep.tile([P, S], F32, name=f"ex{t}", align_bytes=64) for t in range(PACK)]
        ex_plain = [keep.tile([P, S], F32, name=f"ex_plain{t}", align_bytes=64) for t in range(PACK)]

        def weigh(c):
            nc.vector.scalar_tensor_tensor(
                out=z_bf[c][:],
                in0=h_ps[c][:].rearrange("p t n -> p n t"),
                scalar=0.0,
                in1=gs_sb[:].unsqueeze(1).to_broadcast([P, ZW, PACK]),
                op0=ALU.max,
                op1=ALU.mult,
            )

        def weigh_on_scalar(c):
            h_pos = keep.tile([P, PACK, ZW], F32, name=f"h_pos{c}", align_bytes=64)
            z_rows = keep.tile([P, PACK, ZW], BF16, name=f"z_rows{c}", align_bytes=64)
            nc.scalar.activation(out=h_pos[:], in_=h_ps[c][:], func=ACT.Relu)
            for t in range(PACK):
                nc.scalar.activation(out=z_rows[:, t, :], in_=h_pos[:, t, :], func=ACT.Copy, scale=gs_sb[:, t : t + 1])
            nc.scalar.copy(z_bf[c][:].rearrange("p (c i) t -> p c t i", i=4), z_rows[:].rearrange("p t (c i) -> p c t i", i=4))

        def quantise_z(c):
            h, part = divmod(c * ZW, HALF)
            nc.vector.quantize_mx(
                out=z_w[h][:, part : part + ZW].bitcast(FP8X4),
                scales=z_s[h][:, part : part + ZW],
                in_=z_bf[c][:].rearrange("p n t -> p (n t)"),
            )

        def score(h):
            cols = slice(h * HALF, (h + 1) * HALF)
            for t in range(PACK):
                bank = psum.tile([P, HALF], F32, name=f"s_ps{h}{t}", tag=f"bank{(1 - h) * PACK + t}")
                nc.tensor.matmul_mx(
                    out=bank[:],
                    lhsT=cand_w[:, t, :].bitcast(FP8X4),
                    lhsT_scale=cand_s[:, t, :],
                    rhs=z_w[h][:].bitcast(FP8X4),
                    rhs_scale=z_s[h][:],
                    start=True,
                    stop=True,
                )
                nc.scalar.activation(out=ex[t][:, cols], in_=bank[:], func=ACT.Exp, scale=0.5 * 0.0625)
                if h == 1:
                    nc.sync.dma_start(ex_plain[t][:, cols], ex[t][:, cols])

        weigh_on_scalar(3)
        weigh(0)
        weigh(1)
        quantise_z(0)
        quantise_z(1)
        score(0)
        weigh(2)
        quantise_z(3)
        quantise_z(2)
        for t in range(PACK):
            nc.vector.tensor_copy(ex_plain[t][:, :HALF], ex[t][:, :HALF])
        score(1)

        y_w = keep.tile([P, S], U32, name="y_w", align_bytes=64)
        y_s = keep.tile([P, S], U8, name="y_s", align_bytes=64)
        out_rows = out_0.rearrange("(p t) j -> p t j", t=PACK)
        out_words = out_1[0].rearrange("p n t -> p (n t)").bitcast(I32)

        ln_num = keep.tile([P, PACK, S], F32, name="ln_num", align_bytes=64)
        ln_den = keep.tile([P, PACK, S], F32, name="ln_den", align_bytes=64)

        def fetch_n2(h):
            at2 = keep.tile([P, PACK, HALF], F32, name=f"at2_{h}", align_bytes=64)
            for t in range(PACK):
                nc.scalar.activation(out=at2[:, t, :], in_=ex[t][:].indirect(entries(n2_l, h * HALF, HALF)), func=ACT.Copy)
            return at2

        def numerators(h):
            j0 = h * HALF
            num = keep.tile([P, PACK, HALF], F32, name=f"num{h}", align_bytes=64)
            for t in range(PACK):
                nc.vector.tensor_tensor(num[:, t, :], ex[t][:].indirect(entries(n1_l, j0, HALF)), ex_plain[t][:, j0 : j0 + HALF], ALU.add)
            return num

        def denominators(h, at2):
            den = keep.tile([P, PACK, HALF], F32, name=f"den{h}", align_bytes=64)
            for t in range(PACK):
                nc.vector.tensor_tensor(den[:, t, :], ex[t][:].indirect(entries(n3_l, h * HALF, HALF)), at2[:, t, :], ALU.add)
            return den

        def take_logs(ln, sums, j0, first, w):
            nc.scalar.activation(out=ln[:, :, j0 + first : j0 + first + w], in_=sums[:, :, first : first + w], func=ACT.Ln)

        def subtract(j0, w):
            y = keep.tile([P, PACK, w], F32, name=f"y{j0}", align_bytes=64)
            nc.vector.tensor_tensor(y[:], ln_num[:, :, j0 : j0 + w], ln_den[:, :, j0 : j0 + w], ALU.subtract)
            nc.sync.dma_start(out_rows[:, :, j0 : j0 + w], y[:])
            return y

        def interleave(copy, y_bf, y):
            copy(y_bf.rearrange("p (c i) t -> p c t i", i=4), y.rearrange("p t (c i) -> p c t i", i=4))

        def quantise_y(y_bf, j0):
            nc.vector.quantize_mx(
                out=y_w[:, j0 : j0 + HALF].bitcast(FP8X4),
                scales=y_s[:, j0 : j0 + HALF],
                in_=y_bf[:].rearrange("p j t -> p (j t)"),
            )
            nc.sync.dma_start(out_words[:, j0 : j0 + HALF], y_w[:, j0 : j0 + HALF].bitcast(I32))

        y_bf = [keep.tile([P, HALF, PACK], BF16, name=f"y_bf{h}", align_bytes=64) for h in range(2)]
        at2 = [fetch_n2(h) for h in range(2)]
        num0 = numerators(0)
        den0 = denominators(0, at2[0])
        den1 = denominators(1, at2[1])
        num1 = numerators(1)
        take_logs(ln_num, num0, 0, 0, HALF)
        take_logs(ln_den, den0, 0, 0, HALF)
        take_logs(ln_den, den1, HALF, 0, HALF)
        take_logs(ln_num, num1, HALF, 0, ZW)
        take_logs(ln_num, num1, HALF, ZW, ZW)
        y0 = subtract(0, HALF)
        interleave(nc.vector.tensor_copy, y_bf[0][:, :ZW, :], y0[:, :, :ZW])
        y2 = subtract(HALF, ZW)
        y3 = subtract(HALF + ZW, ZW)
        interleave(nc.scalar.copy, y_bf[0][:, ZW:, :], y0[:, :, ZW:])
        interleave(nc.scalar.copy, y_bf[1][:, :ZW, :], y2[:])
        interleave(nc.vector.tensor_copy, y_bf[1][:, ZW:, :], y3[:])
        quantise_y(y_bf[0], 0)
        quantise_y(y_bf[1], HALF)
        for q in range(QUADS):
            eng = nc.sync if q % 2 == 0 else nc.scalar
            eng.dma_start(out_2[0, 4 * q : 4 * q + 4, :].bitcast(I32), y_s[32 * q : 32 * q + 4, :].bitcast(I32))
